import numpy as np
import ml_dtypes


def mxq(x, axis, fmt="e4m3"):
    dtype, down = {"e4m3": (ml_dtypes.float8_e4m3fn, 7), "e5m2": (ml_dtypes.float8_e5m2, 14)}[fmt]
    v = np.moveaxis(np.asarray(x, np.float32).astype(ml_dtypes.bfloat16).astype(np.float64), axis, -1)
    blocks = v.reshape(v.shape[:-1] + (-1, 32))
    amax = np.abs(blocks).max(-1, keepdims=True)
    byte = np.maximum(np.where(amax > 0, np.frexp(amax)[1] - 1 + 127, 0) - down, 1)
    scale = np.exp2(byte - 127.0)
    codes = (blocks / scale).astype(np.float32).astype(dtype).astype(np.float64)
    return np.moveaxis((codes * scale).reshape(v.shape), -1, axis)


WIDE = False


def mx_kscale(k):
    if not WIDE:
        return np.ones(k)
    levels = np.array([10, -10, 5, -5, 0])
    if k % 512:
        return np.exp2(np.random.permutation(np.resize(levels, k // 32))).repeat(32)
    a = np.empty((k // 512, 16))
    for p in range(k // 512):
        a[p, :8] = np.random.permutation(np.resize(levels, 8))
        for g in range(8):
            far = levels[np.abs(levels - a[p, g]) >= 10]
            a[p, g + 8] = far[np.random.randint(len(far))]
    return np.exp2(a.ravel()).repeat(32)


def f64(x):
    return np.asarray(x).astype(np.float64)


def striped8(idx):
    return np.asarray(idx).reshape(8, -1, 16).transpose(0, 2, 1).reshape(128, -1).astype(np.uint16)


def unstriped8(offs):
    return offs.reshape(8, 16, -1).transpose(0, 2, 1).reshape(8, -1).astype(np.int64)


def pick8(x, idx, run):
    r = np.arange(len(x))
    return x[r[:, None], idx[r % (8 * run) // run]]


E2M1 = np.array([0.0, 0.5, 1.0, 1.5, 2.0, 3.0, 4.0, 6.0, -0.0, -0.5, -1.0, -1.5, -2.0, -3.0, -4.0, -6.0])


def pack_weight(w, fmt):
    k, n = w.shape
    w = f64(np.asarray(w, np.float32).astype(ml_dtypes.bfloat16)).reshape(k // 32, 32, n)
    amax = np.abs(w).max(1)
    if fmt == "e4m3":
        byte = np.frexp(amax)[1] - 1 + 127 - 7
    else:
        mant, ex = np.frexp(amax / 6.0)
        byte = np.where(mant > 0.5, ex, ex - 1) + 127
    byte = np.clip(np.where(amax > 0, byte, 1), 1, 254)
    scaled = (w * np.exp2(127.0 - byte)[:, None, :]).reshape(k, n).astype(np.float32)
    by_word = np.ascontiguousarray(scaled.reshape(k // 512, 128, 4, n).transpose(0, 1, 3, 2))
    if fmt == "e4m3":
        words = by_word.astype(ml_dtypes.float8_e4m3fn).view(np.uint8)
    else:
        c = by_word.astype(ml_dtypes.float4_e2m1fn).view(np.uint8) & 0xF
        words = (c[..., 0::2] | (c[..., 1::2] << 4)).reshape(k // 512, 128, 2 * n)
    return np.ascontiguousarray(words), np.ascontiguousarray(byte.astype(np.uint8).reshape(k // 512, 16, n))


def unpack_weight(words, scales, fmt):
    g, _, n = scales.shape
    words = np.ascontiguousarray(words).reshape(g, 128, n, -1)
    if fmt == "e4m3":
        vals = words.view(ml_dtypes.float8_e4m3fn).astype(np.float64)
    else:
        nib = np.empty((g, 128, n, 4), np.uint8)
        nib[..., 0::2] = words & 0xF
        nib[..., 1::2] = words >> 4
        vals = E2M1[nib]
    vals = vals * np.repeat(np.exp2(scales.astype(np.float64) - 127.0), 8, axis=1)[..., None]
    return vals.transpose(0, 1, 3, 2).reshape(g * 512, n)


D, T, U, I, Q = 512, 1024, 1024, 512, 128


def setup_inputs():
    n = np.random.standard_normal
    idx = np.stack([np.random.permutation(U)[:I] for _ in range(8)])
    idx2 = np.stack([np.random.permutation(U)[:I] for _ in range(8)])
    idx3 = np.stack([np.random.permutation(U)[:I] for _ in range(8)])
    idx4 = np.stack([np.random.permutation(T)[:I] for _ in range(8)])
    idx5 = np.stack([np.random.permutation(U)[:I] for _ in range(8)])
    fd = mx_kscale(D)
    cachep = pack_weight(n((D, T)) / fd[:, None], "e4m3")
    draftp = pack_weight(n((D, U)) / fd[:, None], "e2m1")
    return {
        "query": (n((D, Q)) * 1.0 / np.sqrt(D) * fd[:, None]).astype(np.float32),
        "cache_words": cachep[0],
        "cache_scales": cachep[1],
        "draft_words": draftp[0],
        "draft_scales": draftp[1],
        "offs": striped8(idx),
        "offs2": striped8(idx2),
        "offs3": striped8(idx3),
        "offs4": striped8(idx4),
        "offs5": striped8(idx5),
    }


def reference(query, cache_words, cache_scales, draft_words, draft_scales, offs, offs2, offs3, offs4, offs5):
    idx = unstriped8(offs)
    idx2 = unstriped8(offs2)
    idx3 = unstriped8(offs3)
    idx4 = unstriped8(offs4)
    idx5 = unstriped8(offs5)
    cacheu = unpack_weight(cache_words, cache_scales, "e4m3")
    draftu = unpack_weight(draft_words, draft_scales, "e2m1")
    queryq = mxq(f64(query), 0, "e4m3")
    a = queryq.T @ cacheu
    b = queryq.T @ draftu
    nb = np.zeros((Q, U))
    nb[np.arange(Q)[:, None], idx2[np.arange(Q) % 128 // 16]] = pick8(b, idx, 16)
    w = np.maximum(pick8(nb, idx3, 16), pick8(a, idx4, 16))
    n2 = np.zeros((Q, U))
    n2[np.arange(Q)[:, None], idx5[np.arange(Q) % 128 // 16]] = w
    r = n2 - nb
    y = pick8(r, idx3, 16)
    return y

@@ -1,0 +1,150 @@
+from contextlib import ExitStack
+
+import concourse.mybir as mybir
+
+D, T, U, I, Q = 512, 1024, 1024, 512, 128
+FLOPS = 2 * D * Q * (T + U)
+
+F32 = mybir.dt.float32
+BF16 = mybir.dt.bfloat16
+I32 = mybir.dt.int32
+U32 = mybir.dt.uint32
+U16 = mybir.dt.uint16
+U8 = mybir.dt.uint8
+FP8X4 = mybir.dt.float8_e4m3fn_x4
+FP4X4 = mybir.dt.float4_e2m1fn_x4
+COPY = mybir.ActivationFunctionType.Copy
+MAX = mybir.AluOpType.max
+ADD = mybir.AluOpType.add
+SUB = mybir.AluOpType.subtract
+
+P = 128
+PACK = 4
+LANES = 16
+HALF = I // 2
+B_CHUNKS = (256, 256, 256, 128, 128)
+A_CHUNK = 512
+W_FIRST = 128
+
+
+def entries(list_tile, lo, hi):
+    return list_tile[:, lo // LANES : hi // LANES]
+
+
+def load_scale_rows(nc, plane, scales):
+    for quad in range(4):
+        nc.sync.dma_start(
+            plane[32 * quad : 32 * quad + 4, :].bitcast(I32),
+            scales[0, 4 * quad : 4 * quad + 4, :].bitcast(I32),
+        )
+
+
+def tile_attend_beamtwice_two_kernel(
+    tc, query, cache_words, cache_scales, draft_words, draft_scales, offs, offs2, offs3, offs4, offs5, out
+):
+    nc = tc.nc
+    with ExitStack() as ctx:
+        sb = ctx.enter_context(tc.tile_pool(name="sb", bufs=1))
+        psum = ctx.enter_context(tc.psum_pool(name="psum", bufs=1))
+
+        list1 = sb.tile([P, I // LANES], U16, name="list1")
+        list2 = sb.tile([P, I // LANES], U16, name="list2")
+        list3 = sb.tile([P, I // LANES], U16, name="list3")
+        list4 = sb.tile([P, I // LANES], U16, name="list4")
+        list5 = sb.tile([P, I // LANES], U16, name="list5")
+        q_raw = sb.tile([P, PACK, Q], F32, name="q_raw")
+        q_bf = sb.tile([P, Q, PACK], BF16, name="q_bf", tag="q_bf_then_n2_rest", align_bytes=64)
+        q_codes = sb.tile([P, Q], U32, name="q_codes", align_bytes=64)
+        q_plane = sb.tile([P, Q], U8, name="q_plane", align_bytes=64)
+        d_codes = sb.tile([P, 2 * U], U8, name="d_codes", align_bytes=64)
+        d_plane = sb.tile([P, U], U8, name="d_plane", align_bytes=64)
+        c_codes = sb.tile([P, T], I32, name="c_codes", align_bytes=64)
+        c_plane = sb.tile([P, T], U8, name="c_plane", align_bytes=64)
+        a_sb = sb.tile([P, T], F32, name="a_sb", tag="a_then_nb_pick")
+        b_sb = sb.tile([P, U], F32, name="b_sb")
+        nb = sb.tile([P, U], F32, name="nb")
+        n2_first = sb.tile([P, U], F32, name="n2_first")
+        r_part = sb.tile([P, U], F32, name="r_part")
+        r_sb = sb.tile([P, U], F32, name="r_sb")
+        b_pick = sb.tile([P, I], F32, name="b_pick")
+        a_pick = sb.tile([P, I], F32, name="a_pick")
+        w_sb = sb.tile([P, I], F32, name="w_sb")
+        y_sb = sb.tile([P, I], F32, name="y_sb")
+
+        nc.vector.memset(d_plane[:].bitcast(I32), 0)
+        nc.vector.memset(c_plane[:].bitcast(I32), 0)
+        nc.vector.memset(nb[:], 0.0)
+        nc.vector.memset(n2_first[:], 0.0)
+
+        nc.sync.dma_start(q_raw[:], query.rearrange("(p j) q -> p j q", j=PACK))
+        nc.sync.dma_start(d_codes[:].bitcast(I32), draft_words[0].bitcast(I32))
+        load_scale_rows(nc, d_plane, draft_scales)
+        nc.sync.dma_start(list1[:], offs)
+        nc.sync.dma_start(c_codes[:], cache_words[0].rearrange("p t j -> p (t j)").bitcast(I32))
+        nc.sync.dma_start(list2[:], offs2)
+        load_scale_rows(nc, c_plane, cache_scales)
+        nc.sync.dma_start(list4[:], offs4)
+        nc.sync.dma_start(list3[:], offs3)
+        nc.sync.dma_start(list5[:], offs5)
+
+        nc.vector.tensor_copy(q_bf[:], q_raw[:].rearrange("p j q -> p q j"))
+        nc.vector.quantize_mx(
+            out=q_codes[:].bitcast(FP8X4),
+            scales=q_plane[:],
+            in_=q_bf[:].rearrange("p q j -> p (q j)"),
+        )
+
+        n2_rest = sb.tile([P, U], F32, name="n2_rest", tag="q_bf_then_n2_rest", align_bytes=64)
+        nc.vector.memset(n2_rest[:], 0.0)
+
+        lo = 0
+        for n, width in enumerate(B_CHUNKS):
+            hi = lo + width
+            bank = psum.tile([P, width], F32, name="b_bank%d" % n)
+            nc.tensor.matmul_mx(
+                out=bank[:],
+                lhsT=q_codes[:].bitcast(FP8X4),
+                lhsT_scale=q_plane[:],
+                rhs=d_codes[:, 2 * lo : 2 * hi].bitcast(FP4X4),
+                rhs_scale=d_plane[:, lo:hi],
+                start=True,
+                stop=True,
+            )
+            if n % 2 == 0:
+                nc.vector.tensor_copy(b_sb[:, lo:hi], bank[:])
+            else:
+                nc.scalar.activation(b_sb[:, lo:hi], bank[:], COPY)
+            lo = hi
+
+        nc.vector.tensor_copy(b_pick[:, :HALF], b_sb[:].indirect(entries(list1, 0, HALF)))
+        nc.scalar.activation(b_pick[:, HALF:], b_sb[:].indirect(entries(list1, HALF, I)), COPY)
+        nc.scalar.activation(nb[:].indirect(list2[:]), b_pick[:], COPY)
+
+        for n in range(T // A_CHUNK):
+            cols = slice(n * A_CHUNK, (n + 1) * A_CHUNK)
+            bank = psum.tile([P, A_CHUNK], F32, name="a_bank%d" % n)
+            nc.tensor.matmul_mx(
+                out=bank[:],
+                lhsT=q_codes[:].bitcast(FP8X4),
+                lhsT_scale=q_plane[:],
+                rhs=c_codes[:, cols].bitcast(FP8X4),
+                rhs_scale=c_plane[:, cols],
+                start=True,
+                stop=True,
+            )
+            nc.vector.tensor_copy(a_sb[:, cols], bank[:])
+        nc.vector.tensor_copy(a_pick[:], a_sb[:].indirect(list4[:]))
+
+        nb_pick = sb.tile([P, I], F32, name="nb_pick", tag="a_then_nb_pick")
+        nc.vector.tensor_copy(nb_pick[:, :HALF], nb[:].indirect(entries(list3, 0, HALF)))
+        nc.scalar.activation(nb_pick[:, HALF:], nb[:].indirect(entries(list3, HALF, I)), COPY)
+        for n2, lo, hi in ((n2_first, 0, W_FIRST), (n2_rest, W_FIRST, I)):
+            nc.vector.tensor_tensor(w_sb[:, lo:hi], nb_pick[:, lo:hi], a_pick[:, lo:hi], MAX)
+            nc.scalar.activation(n2[:].indirect(entries(list5, lo, hi)), w_sb[:, lo:hi], COPY)
+
+        nc.vector.tensor_tensor(r_part[:], n2_first[:], nb[:], SUB)
+        nc.vector.tensor_tensor(r_sb[:], n2_rest[:], r_part[:], ADD)
+        nc.vector.tensor_copy(y_sb[:, :HALF], r_sb[:].indirect(entries(list3, 0, HALF)))
+        nc.scalar.activation(y_sb[:, HALF:], r_sb[:].indirect(entries(list3, HALF, I)), COPY)
+        nc.sync.dma_start(out[:, :HALF], y_sb[:, :HALF])
+        nc.scalar.dma_start(out[:, HALF:], y_sb[:, HALF:])

@@ -24,7 +24,7 @@ LANES = 16
 HALF = I // 2
 B_CHUNKS = (256, 256, 256, 128, 128)
 A_CHUNK = 512
-W_FIRST = 128
+W_FIRST = 96
 
 
 def entries(list_tile, lo, hi):
@@ -56,7 +56,7 @@ def tile_attend_beamtwice_two_kernel(
         q_bf = sb.tile([P, Q, PACK], BF16, name="q_bf", tag="q_bf_then_n2_rest", align_bytes=64)
         q_codes = sb.tile([P, Q], U32, name="q_codes", align_bytes=64)
         q_plane = sb.tile([P, Q], U8, name="q_plane", align_bytes=64)
-        d_codes = sb.tile([P, 2 * U], U8, name="d_codes", align_bytes=64)
+        d_codes = [sb.tile([P, U], U8, name="d_codes%d" % n, align_bytes=64) for n in range(2)]
         d_plane = sb.tile([P, U], U8, name="d_plane", align_bytes=64)
         c_codes = sb.tile([P, T], I32, name="c_codes", align_bytes=64)
         c_plane = sb.tile([P, T], U8, name="c_plane", align_bytes=64)
@@ -77,22 +77,32 @@ def tile_attend_beamtwice_two_kernel(
         nc.vector.memset(n2_first[:], 0.0)
 
         nc.sync.dma_start(q_raw[:], query.rearrange("(p j) q -> p j q", j=PACK))
-        nc.sync.dma_start(d_codes[:].bitcast(I32), draft_words[0].bitcast(I32))
+        nc.sync.dma_start(d_codes[0][:].bitcast(I32), draft_words[0, :, :U].bitcast(I32))
         load_scale_rows(nc, d_plane, draft_scales)
-        nc.sync.dma_start(list1[:], offs)
+        nc.sync.dma_start(d_codes[1][:].bitcast(I32), draft_words[0, :, U:].bitcast(I32))
         nc.sync.dma_start(c_codes[:], cache_words[0].rearrange("p t j -> p (t j)").bitcast(I32))
-        nc.sync.dma_start(list2[:], offs2)
+        nc.sync.dma_start(list1[:], offs)
         load_scale_rows(nc, c_plane, cache_scales)
+        nc.sync.dma_start(list2[:], offs2)
         nc.sync.dma_start(list4[:], offs4)
         nc.sync.dma_start(list3[:], offs3)
         nc.sync.dma_start(list5[:], offs5)
 
-        nc.vector.tensor_copy(q_bf[:], q_raw[:].rearrange("p j q -> p q j"))
-        nc.vector.quantize_mx(
-            out=q_codes[:].bitcast(FP8X4),
-            scales=q_plane[:],
-            in_=q_bf[:].rearrange("p q j -> p (q j)"),
-        )
+        def round_rows(copy, lo, hi):
+            copy(
+                q_bf[:, lo:hi, :].rearrange("p (c i) j -> p c j i", i=4),
+                q_raw[:, :, lo:hi].rearrange("p j (c i) -> p c j i", i=4),
+            )
+
+        round_rows(nc.vector.tensor_copy, 0, 64)
+        round_rows(nc.vector.tensor_copy, 64, 96)
+        round_rows(nc.scalar.copy, 96, 128)
+        for lo, hi in ((0, 64), (64, 128)):
+            nc.vector.quantize_mx(
+                out=q_codes[:, lo:hi].bitcast(FP8X4),
+                scales=q_plane[:, lo:hi],
+                in_=q_bf[:, lo:hi, :].rearrange("p q j -> p (q j)"),
+            )
 
         n2_rest = sb.tile([P, U], F32, name="n2_rest", tag="q_bf_then_n2_rest", align_bytes=64)
         nc.vector.memset(n2_rest[:], 0.0)
@@ -105,7 +115,7 @@ def tile_attend_beamtwice_two_kernel(
                 out=bank[:],
                 lhsT=q_codes[:].bitcast(FP8X4),
                 lhsT_scale=q_plane[:],
-                rhs=d_codes[:, 2 * lo : 2 * hi].bitcast(FP4X4),
+                rhs=d_codes[lo // 512][:, 2 * (lo % 512) : 2 * (lo % 512 + width)].bitcast(FP4X4),
                 rhs_scale=d_plane[:, lo:hi],
                 start=True,
                 stop=True,

@@ -1,6 +1,7 @@
 from contextlib import ExitStack
 
 import concourse.mybir as mybir
+from concourse.masks import make_identity
 
 D, T, U, I, Q = 512, 1024, 1024, 512, 128
 FLOPS = 2 * D * Q * (T + U)
@@ -25,6 +26,9 @@ HALF = I // 2
 B_CHUNKS = (256, 256, 256, 128, 128)
 A_CHUNK = 512
 W_FIRST = 96
+BANK = 512
+TURNED = 768
+V_SHARE = 704
 
 
 def entries(list_tile, lo, hi):
@@ -61,10 +65,12 @@ def tile_attend_beamtwice_two_kernel(
         c_codes = sb.tile([P, T], I32, name="c_codes", align_bytes=64)
         c_plane = sb.tile([P, T], U8, name="c_plane", align_bytes=64)
         a_sb = sb.tile([P, T], F32, name="a_sb", tag="a_then_nb_pick")
-        b_sb = sb.tile([P, U], F32, name="b_sb")
+        b_sb = sb.tile([P, U], F32, name="b_sb", tag="b_then_ident")
         nb = sb.tile([P, U], F32, name="nb")
         n2_first = sb.tile([P, U], F32, name="n2_first")
-        r_part = sb.tile([P, U], F32, name="r_part")
+        r_part = sb.tile([P, U - V_SHARE], F32, name="r_part")
+        nb_t = sb.tile([P, TURNED], F32, name="nb_t")
+        part_t = sb.tile([P, TURNED], F32, name="part_t")
         r_sb = sb.tile([P, U], F32, name="r_sb")
         b_pick = sb.tile([P, I], F32, name="b_pick")
         a_pick = sb.tile([P, I], F32, name="a_pick")
@@ -110,7 +116,7 @@ def tile_attend_beamtwice_two_kernel(
         lo = 0
         for n, width in enumerate(B_CHUNKS):
             hi = lo + width
-            bank = psum.tile([P, width], F32, name="b_bank%d" % n)
+            bank = psum.tile([P, width], F32, name="b_bank%d" % n, tag="bank%d" % n)
             nc.tensor.matmul_mx(
                 out=bank[:],
                 lhsT=q_codes[:].bitcast(FP8X4),
@@ -130,9 +136,12 @@ def tile_attend_beamtwice_two_kernel(
         nc.scalar.activation(b_pick[:, HALF:], b_sb[:].indirect(entries(list1, HALF, I)), COPY)
         nc.scalar.activation(nb[:].indirect(list2[:]), b_pick[:], COPY)
 
+        ident = sb.tile([P, P], F32, name="ident", tag="b_then_ident")
+        make_identity(nc, ident[:])
+
         for n in range(T // A_CHUNK):
             cols = slice(n * A_CHUNK, (n + 1) * A_CHUNK)
-            bank = psum.tile([P, A_CHUNK], F32, name="a_bank%d" % n)
+            bank = psum.tile([P, A_CHUNK], F32, name="a_bank%d" % n, tag="bank%d" % (5 + n))
             nc.tensor.matmul_mx(
                 out=bank[:],
                 lhsT=q_codes[:].bitcast(FP8X4),
@@ -152,8 +161,28 @@ def tile_attend_beamtwice_two_kernel(
             nc.vector.tensor_tensor(w_sb[:, lo:hi], nb_pick[:, lo:hi], a_pick[:, lo:hi], MAX)
             nc.scalar.activation(n2[:].indirect(entries(list5, lo, hi)), w_sb[:, lo:hi], COPY)
 
-        nc.vector.tensor_tensor(r_part[:], n2_first[:], nb[:], SUB)
-        nc.vector.tensor_tensor(r_sb[:], n2_rest[:], r_part[:], ADD)
+        def turn(bank, bank_lo, src, lo, hi):
+            for c in range(lo, hi, P):
+                nc.tensor.transpose(bank[:, c - bank_lo : c - bank_lo + P], src[:, c : c + P], ident[:])
+
+        for n, lo in enumerate(range(0, TURNED, BANK)):
+            hi = min(lo + BANK, TURNED)
+            bank = psum.tile([P, hi - lo], F32, name="nb_t_bank%d" % n, tag="bank%d" % n)
+            turn(bank, lo, nb, lo, hi)
+            nc.vector.tensor_copy(nb_t[:, lo:hi], bank[:])
+        nc.gpsimd.tensor_tensor(r_part[:], n2_first[:, V_SHARE:], nb[:, V_SHARE:], SUB)
+        for n, lo in enumerate(range(0, TURNED, 2 * P)):
+            hi = lo + 2 * P
+            bank = psum.tile([P, 2 * P], F32, name="n2_t_bank%d" % n, tag="bank%d" % (2 + n))
+            turn(bank, lo, n2_first, lo, hi)
+            nc.vector.tensor_tensor(part_t[:, lo:hi], bank[:], nb_t[:, lo:hi], SUB)
+        for n, lo in enumerate(range(0, TURNED, BANK)):
+            hi = min(lo + BANK, TURNED)
+            bank = psum.tile([P, hi - lo], F32, name="part_bank%d" % n, tag="bank%d" % (5 + n))
+            turn(bank, lo, part_t, lo, hi)
+            end = min(hi, V_SHARE)
+            nc.vector.tensor_tensor(r_sb[:, lo:end], bank[:, : end - lo], n2_rest[:, lo:end], ADD)
+        nc.gpsimd.tensor_tensor(r_sb[:, V_SHARE:], n2_rest[:, V_SHARE:], r_part[:], ADD)
         nc.vector.tensor_copy(y_sb[:, :HALF], r_sb[:].indirect(entries(list3, 0, HALF)))
         nc.scalar.activation(y_sb[:, HALF:], r_sb[:].indirect(entries(list3, HALF, I)), COPY)
         nc.sync.dma_start(out[:, :HALF], y_sb[:, :HALF])

from contextlib import ExitStack

import concourse.mybir as mybir
from concourse.masks import make_identity

D, T, U, I, Q = 512, 1024, 1024, 512, 128
FLOPS = 2 * D * Q * (T + U)

F32 = mybir.dt.float32
BF16 = mybir.dt.bfloat16
I32 = mybir.dt.int32
U32 = mybir.dt.uint32
U16 = mybir.dt.uint16
U8 = mybir.dt.uint8
FP8X4 = mybir.dt.float8_e4m3fn_x4
FP4X4 = mybir.dt.float4_e2m1fn_x4
COPY = mybir.ActivationFunctionType.Copy
MAX = mybir.AluOpType.max
ADD = mybir.AluOpType.add
SUB = mybir.AluOpType.subtract

P = 128
PACK = 4
LANES = 16
HALF = I // 2
B_CHUNKS = (256, 256, 256, 128, 128)
A_CHUNK = 512
W_FIRST = 96
BANK = 512
TURNED = 768
V_SHARE = 704


def entries(list_tile, lo, hi):
    return list_tile[:, lo // LANES : hi // LANES]


def load_scale_rows(nc, plane, scales):
    for quad in range(4):
        nc.sync.dma_start(
            plane[32 * quad : 32 * quad + 4, :].bitcast(I32),
            scales[0, 4 * quad : 4 * quad + 4, :].bitcast(I32),
        )


def tile_attend_beamtwice_two_kernel(
    tc, query, cache_words, cache_scales, draft_words, draft_scales, offs, offs2, offs3, offs4, offs5, out
):
    nc = tc.nc
    with ExitStack() as ctx:
        sb = ctx.enter_context(tc.tile_pool(name="sb", bufs=1))
        psum = ctx.enter_context(tc.psum_pool(name="psum", bufs=1))

        list1 = sb.tile([P, I // LANES], U16, name="list1")
        list2 = sb.tile([P, I // LANES], U16, name="list2")
        list3 = sb.tile([P, I // LANES], U16, name="list3")
        list4 = sb.tile([P, I // LANES], U16, name="list4")
        list5 = sb.tile([P, I // LANES], U16, name="list5")
        q_raw = sb.tile([P, PACK, Q], F32, name="q_raw")
        q_bf = sb.tile([P, Q, PACK], BF16, name="q_bf", tag="q_bf_then_n2_rest", align_bytes=64)
        q_codes = sb.tile([P, Q], U32, name="q_codes", align_bytes=64)
        q_plane = sb.tile([P, Q], U8, name="q_plane", align_bytes=64)
        d_codes = [sb.tile([P, U], U8, name="d_codes%d" % n, align_bytes=64) for n in range(2)]
        d_plane = sb.tile([P, U], U8, name="d_plane", align_bytes=64)
        c_codes = sb.tile([P, T], I32, name="c_codes", align_bytes=64)
        c_plane = sb.tile([P, T], U8, name="c_plane", align_bytes=64)
        a_sb = sb.tile([P, T], F32, name="a_sb", tag="a_then_nb_pick")
        b_sb = sb.tile([P, U], F32, name="b_sb", tag="b_then_ident")
        nb = sb.tile([P, U], F32, name="nb")
        n2_first = sb.tile([P, U], F32, name="n2_first")
        r_part = sb.tile([P, U - V_SHARE], F32, name="r_part")
        nb_t = sb.tile([P, TURNED], F32, name="nb_t")
        part_t = sb.tile([P, TURNED], F32, name="part_t")
        r_sb = sb.tile([P, U], F32, name="r_sb")
        b_pick = sb.tile([P, I], F32, name="b_pick")
        a_pick = sb.tile([P, I], F32, name="a_pick")
        w_sb = sb.tile([P, I], F32, name="w_sb")
        y_sb = sb.tile([P, I], F32, name="y_sb")

        nc.vector.memset(d_plane[:].bitcast(I32), 0)
        nc.vector.memset(c_plane[:].bitcast(I32), 0)
        nc.vector.memset(nb[:], 0.0)
        nc.vector.memset(n2_first[:], 0.0)

        nc.sync.dma_start(q_raw[:], query.rearrange("(p j) q -> p j q", j=PACK))
        nc.sync.dma_start(d_codes[0][:].bitcast(I32), draft_words[0, :, :U].bitcast(I32))
        load_scale_rows(nc, d_plane, draft_scales)
        nc.sync.dma_start(d_codes[1][:].bitcast(I32), draft_words[0, :, U:].bitcast(I32))
        nc.sync.dma_start(c_codes[:], cache_words[0].rearrange("p t j -> p (t j)").bitcast(I32))
        nc.sync.dma_start(list1[:], offs)
        load_scale_rows(nc, c_plane, cache_scales)
        nc.sync.dma_start(list2[:], offs2)
        nc.sync.dma_start(list4[:], offs4)
        nc.sync.dma_start(list3[:], offs3)
        nc.sync.dma_start(list5[:], offs5)

        def round_rows(copy, lo, hi):
            copy(
                q_bf[:, lo:hi, :].rearrange("p (c i) j -> p c j i", i=4),
                q_raw[:, :, lo:hi].rearrange("p j (c i) -> p c j i", i=4),
            )

        round_rows(nc.vector.tensor_copy, 0, 64)
        round_rows(nc.vector.tensor_copy, 64, 96)
        round_rows(nc.scalar.copy, 96, 128)
        for lo, hi in ((0, 64), (64, 128)):
            nc.vector.quantize_mx(
                out=q_codes[:, lo:hi].bitcast(FP8X4),
                scales=q_plane[:, lo:hi],
                in_=q_bf[:, lo:hi, :].rearrange("p q j -> p (q j)"),
            )

        n2_rest = sb.tile([P, U], F32, name="n2_rest", tag="q_bf_then_n2_rest", align_bytes=64)
        nc.vector.memset(n2_rest[:], 0.0)

        lo = 0
        for n, width in enumerate(B_CHUNKS):
            hi = lo + width
            bank = psum.tile([P, width], F32, name="b_bank%d" % n, tag="bank%d" % n)
            nc.tensor.matmul_mx(
                out=bank[:],
                lhsT=q_codes[:].bitcast(FP8X4),
                lhsT_scale=q_plane[:],
                rhs=d_codes[lo // 512][:, 2 * (lo % 512) : 2 * (lo % 512 + width)].bitcast(FP4X4),
                rhs_scale=d_plane[:, lo:hi],
                start=True,
                stop=True,
            )
            if n % 2 == 0:
                nc.vector.tensor_copy(b_sb[:, lo:hi], bank[:])
            else:
                nc.scalar.activation(b_sb[:, lo:hi], bank[:], COPY)
            lo = hi

        nc.vector.tensor_copy(b_pick[:, :HALF], b_sb[:].indirect(entries(list1, 0, HALF)))
        nc.scalar.activation(b_pick[:, HALF:], b_sb[:].indirect(entries(list1, HALF, I)), COPY)
        nc.scalar.activation(nb[:].indirect(list2[:]), b_pick[:], COPY)

        ident = sb.tile([P, P], F32, name="ident", tag="b_then_ident")
        make_identity(nc, ident[:])

        for n in range(T // A_CHUNK):
            cols = slice(n * A_CHUNK, (n + 1) * A_CHUNK)
            bank = psum.tile([P, A_CHUNK], F32, name="a_bank%d" % n, tag="bank%d" % (5 + n))
            nc.tensor.matmul_mx(
                out=bank[:],
                lhsT=q_codes[:].bitcast(FP8X4),
                lhsT_scale=q_plane[:],
                rhs=c_codes[:, cols].bitcast(FP8X4),
                rhs_scale=c_plane[:, cols],
                start=True,
                stop=True,
            )
            nc.vector.tensor_copy(a_sb[:, cols], bank[:])
        nc.vector.tensor_copy(a_pick[:], a_sb[:].indirect(list4[:]))

        nb_pick = sb.tile([P, I], F32, name="nb_pick", tag="a_then_nb_pick")
        nc.vector.tensor_copy(nb_pick[:, :HALF], nb[:].indirect(entries(list3, 0, HALF)))
        nc.scalar.activation(nb_pick[:, HALF:], nb[:].indirect(entries(list3, HALF, I)), COPY)
        for n2, lo, hi in ((n2_first, 0, W_FIRST), (n2_rest, W_FIRST, I)):
            nc.vector.tensor_tensor(w_sb[:, lo:hi], nb_pick[:, lo:hi], a_pick[:, lo:hi], MAX)
            nc.scalar.activation(n2[:].indirect(entries(list5, lo, hi)), w_sb[:, lo:hi], COPY)

        def turn(bank, bank_lo, src, lo, hi):
            for c in range(lo, hi, P):
                nc.tensor.transpose(bank[:, c - bank_lo : c - bank_lo + P], src[:, c : c + P], ident[:])

        for n, lo in enumerate(range(0, TURNED, BANK)):
            hi = min(lo + BANK, TURNED)
            bank = psum.tile([P, hi - lo], F32, name="nb_t_bank%d" % n, tag="bank%d" % n)
            turn(bank, lo, nb, lo, hi)
            nc.vector.tensor_copy(nb_t[:, lo:hi], bank[:])
        nc.gpsimd.tensor_tensor(r_part[:], n2_first[:, V_SHARE:], nb[:, V_SHARE:], SUB)
        for n, lo in enumerate(range(0, TURNED, 2 * P)):
            hi = lo + 2 * P
            bank = psum.tile([P, 2 * P], F32, name="n2_t_bank%d" % n, tag="bank%d" % (2 + n))
            turn(bank, lo, n2_first, lo, hi)
            nc.vector.tensor_tensor(part_t[:, lo:hi], bank[:], nb_t[:, lo:hi], SUB)
        for n, lo in enumerate(range(0, TURNED, BANK)):
            hi = min(lo + BANK, TURNED)
            bank = psum.tile([P, hi - lo], F32, name="part_bank%d" % n, tag="bank%d" % (5 + n))
            turn(bank, lo, part_t, lo, hi)
            end = min(hi, V_SHARE)
            nc.vector.tensor_tensor(r_sb[:, lo:end], bank[:, : end - lo], n2_rest[:, lo:end], ADD)
        nc.gpsimd.tensor_tensor(r_sb[:, V_SHARE:], n2_rest[:, V_SHARE:], r_part[:], ADD)
        nc.vector.tensor_copy(y_sb[:, :HALF], r_sb[:].indirect(entries(list3, 0, HALF)))
        nc.scalar.activation(y_sb[:, HALF:], r_sb[:].indirect(entries(list3, HALF, I)), COPY)
        nc.sync.dma_start(out[:, :HALF], y_sb[:, :HALF])
        nc.scalar.dma_start(out[:, HALF:], y_sb[:, HALF:])
